import numpy as np
import ml_dtypes


def mxq(x, axis, fmt="e4m3"):
    dtype, down = {"e4m3": (ml_dtypes.float8_e4m3fn, 7), "e5m2": (ml_dtypes.float8_e5m2, 14)}[fmt]
    v = np.moveaxis(np.asarray(x, np.float32).astype(ml_dtypes.bfloat16).astype(np.float64), axis, -1)
    blocks = v.reshape(v.shape[:-1] + (-1, 32))
    amax = np.abs(blocks).max(-1, keepdims=True)
    byte = np.maximum(np.where(amax > 0, np.frexp(amax)[1] - 1 + 127, 0) - down, 1)
    scale = np.exp2(byte - 127.0)
    codes = (blocks / scale).astype(np.float32).astype(dtype).astype(np.float64)
    return np.moveaxis((codes * scale).reshape(v.shape), -1, axis)


WIDE = False


def mx_kscale(k):
    if not WIDE:
        return np.ones(k)
    levels = np.array([10, -10, 5, -5, 0])
    if k % 512:
        return np.exp2(np.random.permutation(np.resize(levels, k // 32))).repeat(32)
    a = np.empty((k // 512, 16))
    for p in range(k // 512):
        a[p, :8] = np.random.permutation(np.resize(levels, 8))
        for g in range(8):
            far = levels[np.abs(levels - a[p, g]) >= 10]
            a[p, g + 8] = far[np.random.randint(len(far))]
    return np.exp2(a.ravel()).repeat(32)


def f64(x):
    return np.asarray(x).astype(np.float64)


def striped(idx):
    return np.tile(idx.reshape(-1, 16).T, (8, 1)).astype(np.uint16)


def unstriped(offs):
    return offs[:16].T.reshape(-1).astype(np.int64)


def striped8(idx):
    return np.concatenate([x.reshape(-1, 16).T for x in idx]).astype(np.uint16)


def runs(offs, k):
    lists = np.stack([offs[16 * r : 16 * r + 16].T.reshape(-1) for r in range(8)]).astype(np.int64)
    return lists[np.arange(k) % 512 // 64]


def pack_weight(w):
    k, n = w.shape
    w = f64(np.asarray(w, np.float32).astype(ml_dtypes.bfloat16)).reshape(k // 32, 32, n)
    amax = np.abs(w).max(1)
    byte = np.clip(np.where(amax > 0, np.frexp(amax)[1] - 1 + 127 - 7, 1), 1, 254)
    scaled = (w * np.exp2(127.0 - byte)[:, None, :]).reshape(k, n).astype(np.float32)
    words = np.ascontiguousarray(scaled.reshape(k // 512, 128, 4, n).transpose(0, 1, 3, 2)).astype(ml_dtypes.float8_e4m3fn).view(np.uint8)
    return words, np.ascontiguousarray(byte.astype(np.uint8).reshape(k // 512, 16, n))


def unpack_weight(words, scales):
    g, p, n, _ = words.shape
    vals = np.ascontiguousarray(words).view(ml_dtypes.float8_e4m3fn).astype(np.float64) * np.repeat(np.exp2(scales.astype(np.float64) - 127.0), 8, axis=1)[..., None]
    return vals.transpose(0, 1, 3, 2).reshape(g * 512, n)


E2M1 = np.array([0.0, 0.5, 1.0, 1.5, 2.0, 3.0, 4.0, 6.0, -0.0, -0.5, -1.0, -1.5, -2.0, -3.0, -4.0, -6.0])


def pack_fp4(w):
    k, n = w.shape
    w = f64(np.asarray(w, np.float32).astype(ml_dtypes.bfloat16)).reshape(k // 32, 32, n)
    amax = np.abs(w).max(1)
    mant, ex = np.frexp(amax / 6.0)
    byte = np.clip(np.where(amax > 0, np.where(mant > 0.5, ex, ex - 1) + 127, 1), 1, 254)
    scaled = (w * np.exp2(127.0 - byte)[:, None, :]).reshape(k, n).astype(np.float32)
    c = np.ascontiguousarray(scaled.reshape(k // 512, 128, 4, n).transpose(0, 1, 3, 2)).astype(ml_dtypes.float4_e2m1fn).view(np.uint8) & 0xF
    words = (c[..., 0::2] | (c[..., 1::2] << 4)).reshape(k // 512, 128, 2 * n)
    return np.ascontiguousarray(words), np.ascontiguousarray(byte.astype(np.uint8).reshape(k // 512, 16, n))


def unpack_fp4(words, scales):
    g, _, n = scales.shape
    words = np.ascontiguousarray(words).reshape(g, 128, n, 2)
    nib = np.empty((g, 128, n, 4), np.uint8)
    nib[..., 0::2] = words & 0xF
    nib[..., 1::2] = words >> 4
    vals = E2M1[nib] * np.repeat(np.exp2(scales.astype(np.float64) - 127.0), 8, axis=1)[..., None]
    return vals.transpose(0, 1, 3, 2).reshape(g * 512, n)


def planes(y):
    n, m = y.shape
    v = y.astype(np.float32).astype(ml_dtypes.bfloat16).astype(np.float64).reshape(n // 32, 32, m)
    top = np.abs(v).max(1)
    byte = np.clip(np.where(top > 0, np.frexp(top)[1] - 1 + 127 - 7, 1), 1, 254)
    codes = (v * np.exp2(127.0 - byte)[:, None, :]).reshape(n, m).astype(np.float32).astype(ml_dtypes.float8_e4m3fn).view(np.uint8)
    words = codes.reshape(n // 512, 128, 4, m).transpose(0, 1, 3, 2)
    return np.ascontiguousarray(words), np.ascontiguousarray(byte.astype(np.uint8).reshape(n // 512, 16, m))


K, T, S, N, G, H, W = 512, 2048, 256, 512, 2048, 512, 128


def setup_inputs():
    n = np.random.standard_normal
    s = mx_kscale(K)[:, None]
    u = mx_kscale(K)
    packed_xT = pack_weight(n((K, T)) * s)
    packed_dT = pack_weight(n((K, G)) / s)
    packed_w1 = pack_fp4(n((H, N)) / np.sqrt(H) / u[:, None])
    perm = np.random.permutation(S)
    return {
        "x_words": packed_xT[0],
        "x_scales": packed_xT[1],
        "d_words": packed_dT[0],
        "d_scales": packed_dT[1],
        "gn": (np.random.uniform(0.5, 1.5, (H, 1)) * u[:, None]).astype(np.float32),
        "w1_words": packed_w1[0],
        "w1_scales": packed_w1[1],
        "offs": striped(np.random.permutation(T)[:S]),
        "kidx": striped8(np.random.randint(0, G, (8, H))),
        "n1": striped(perm[:W]),
        "n2": striped(perm[W:]),
        "n3": striped(np.random.permutation(S)),
        "n4": striped(np.random.permutation(S)),
        "n5": striped(np.random.permutation(S)),
    }


def reference(x_words, x_scales, d_words, d_scales, gn, w1_words, w1_scales, offs, kidx, n1, n2, n3, n4, n5):
    d_kidx = unpack_weight(d_words, d_scales)[np.arange(K)[:, None], runs(kidx, K)]
    xq = unpack_weight(x_words, x_scales)[:, unstriped(offs)]
    s = 0.0625 * (d_kidx.T @ xq)
    pa = s[:, unstriped(n1)]
    pb = s[:, unstriped(n2)]
    rb = pa * pb
    ra = pa + pb
    ds = np.zeros((H, S))
    ds[:, unstriped(n1)] = ra
    dt = ds.copy()
    dt[:, unstriped(n2)] = rb
    z = f64(gn) * dt
    h = unpack_fp4(w1_words, w1_scales).T @ mxq(z, 0, "e4m3")
    b1 = h[:, unstriped(n3)]
    b2 = h[:, unstriped(n4)]
    b3 = h[:, unstriped(n5)]
    out_0 = np.maximum(np.maximum(b1, b2), b3) - (0.5 * (np.maximum(np.minimum(b1, b2), np.minimum(np.maximum(b1, b2), b3))))
    return (out_0,) + planes(out_0)

@@ -1,0 +1,207 @@
+from contextlib import ExitStack
+
+import concourse.mybir as mybir
+
+K, T, S, N, G, H, W = 512, 2048, 256, 512, 2048, 512, 128
+P = 128
+PACK = 4
+FLOPS = 2 * K * H * S + 2 * H * N * S
+
+F32 = mybir.dt.float32
+BF16 = mybir.dt.bfloat16
+I32 = mybir.dt.int32
+U32 = mybir.dt.uint32
+U16 = mybir.dt.uint16
+U8 = mybir.dt.uint8
+FP8X4 = mybir.dt.float8_e4m3fn_x4
+FP4X4 = mybir.dt.float4_e2m1fn_x4
+ALU = mybir.AluOpType
+COPY = mybir.ActivationFunctionType.Copy
+
+H_WINDOW = 352
+HALF = S // 2
+HALVES = (slice(0, HALF), slice(HALF, S))
+LAST = PACK - 1
+
+
+def tile_picked_keybondtop2_none_po_kernel(
+    tc, x_words, x_scales, d_words, d_scales, gn, w1_words, w1_scales, offs, kidx, n1, n2, n3, n4, n5, out_0, out_1, out_2
+):
+    nc = tc.nc
+    with ExitStack() as ctx:
+        lists = ctx.enter_context(tc.tile_pool(name="lists", bufs=1))
+        sb = ctx.enter_context(tc.tile_pool(name="sb", bufs=1))
+        ps = ctx.enter_context(tc.psum_pool(name="ps", bufs=1))
+
+        def tile(name, shape, dtype, tag=None):
+            return sb.tile(shape, dtype, name=name, tag=tag or name, align_bytes=64)
+
+        def load_list(name, dram):
+            held = lists.tile(list(dram.shape), U16, name=name)
+            nc.sync.dma_start(held[:], dram)
+            return held
+
+        d_word_table = tile("d_word_table", [P, G], U32)
+        x_word_table = tile("x_word_table", [P, T], U32, "x_table_then_w_words")
+        d_byte_table = tile("d_byte_table", [P, G], U8)
+        x_byte_table = tile("x_byte_table", [P, T], U8)
+
+        nc.gpsimd.memset(d_byte_table[:].bitcast(I32), 0)
+        nc.vector.memset(x_byte_table[:].bitcast(I32), 0)
+        kidx_l = load_list("kidx_l", kidx)
+        gn_raw = tile("gn_raw", [P, PACK], F32)
+        nc.scalar.dma_start(gn_raw[:], gn.rearrange("(p t) o -> p (t o)", t=PACK))
+        for a in range(2):
+            nc.scalar.dma_start(d_byte_table[a:P:16, :].bitcast(I32), d_scales[0][a:16:2, :].bitcast(I32))
+        for q in range(4):
+            nc.scalar.dma_start(x_byte_table[32 * q : 32 * q + 4, :].bitcast(I32), x_scales[0][4 * q : 4 * q + 4, :].bitcast(I32))
+        offs_l = load_list("offs_l", offs)
+        nc.sync.dma_start(d_word_table[:].bitcast(I32), d_words[0].rearrange("p c r -> p (c r)").bitcast(I32))
+        n1_l = load_list("n1_l", n1)
+        n2_l = load_list("n2_l", n2)
+        nc.sync.dma_start(x_word_table[:].bitcast(I32), x_words[0].rearrange("p c r -> p (c r)").bitcast(I32))
+        n3_l = load_list("n3_l", n3)
+        n4_l = load_list("n4_l", n4)
+        n5_l = load_list("n5_l", n5)
+
+        d_bytes_picked = tile("d_bytes_picked", [P, H], U8)
+        nc.vector.tensor_copy(d_bytes_picked[:], d_byte_table[:].indirect(kidx_l[:]))
+        d_bytes_dealt = tile("d_bytes_dealt", [P, H], U8)
+        nc.vector.tensor_copy(
+            d_bytes_dealt[:].rearrange("p (t m) -> p t m", t=PACK), d_bytes_picked[:].rearrange("p (m t) -> p t m", t=PACK)
+        )
+        d_bytes = tile("d_bytes", [P, H], U8, "d_bytes_then_w_bytes")
+        nc.vector.tensor_copy(d_bytes[:].bitcast(I32), d_bytes_dealt[:].bitcast(I32))
+        for a in range(2):
+            nc.sync.dma_start(d_bytes[2 + a : P : 32, :].bitcast(I32), d_bytes_dealt[16 + a : P : 32, :].bitcast(I32))
+
+        d_words_picked = tile("d_words_picked", [P, H], U32)
+        nc.vector.tensor_copy(d_words_picked[:], d_word_table[:].indirect(kidx_l[:]))
+        d_codes = tile("d_codes", [P, H], U32)
+        nc.vector.tensor_copy(
+            d_codes[:].bitcast(I32).rearrange("p (t m) -> p t m", t=PACK),
+            d_words_picked[:].bitcast(I32).rearrange("p (m t) -> p t m", t=PACK),
+        )
+        x_bytes = tile("x_bytes", [P, S], U8)
+        nc.vector.tensor_copy(x_bytes[:], x_byte_table[:].indirect(offs_l[:]))
+        x_codes = tile("x_codes", [P, S], U32)
+        nc.vector.tensor_copy(x_codes[:], x_word_table[:].indirect(offs_l[:]))
+
+        gn16 = tile("gn16", [P, PACK], F32)
+        nc.scalar.activation(gn16[:], gn_raw[:], COPY, scale=0.0625)
+
+        h_rows = [tile("h_rows%d" % t, [P, H_WINDOW], F32) for t in range(PACK)]
+        for t in range(PACK):
+            nc.gpsimd.memset(h_rows[t][:, S:], 0.0)
+
+        def product(name, lhs_codes, lhs_bytes, rhs_codes, rhs_bytes, rows, on_scalar):
+            for t in range(PACK):
+                for part, cols in enumerate(HALVES if t == 0 else (slice(0, S),)):
+                    tag = "first%d" % part if t == 0 else "%s%d" % (name, t)
+                    bank = ps.tile([P, cols.stop - cols.start], F32, name="%s_bank%d_%d" % (name, t, part), tag=tag)
+                    nc.tensor.matmul_mx(
+                        bank[:], lhsT=lhs_codes(t), lhsT_scale=lhs_bytes[:, P * t : P * (t + 1)],
+                        rhs=rhs_codes[:, cols].bitcast(FP8X4), rhs_scale=rhs_bytes[:, cols], start=True, stop=True,
+                    )
+                    if (t, part) in on_scalar:
+                        nc.scalar.copy(rows[t][:, cols], bank[:])
+                    else:
+                        nc.vector.tensor_copy(rows[t][:, cols], bank[:])
+
+        s_rows = [tile("s_rows%d" % t, [P, S], F32) for t in range(PACK)]
+        product("s", lambda t: d_codes[:, P * t : P * (t + 1)].bitcast(FP8X4), d_bytes, x_codes, x_bytes, s_rows, [(0, 0)])
+
+        w_words_raw = tile("w_words_raw", [P, 2 * N], U8, "x_table_then_w_words")
+        w_bytes_raw = tile("w_bytes_raw", [P, N], U8, "d_bytes_then_w_bytes")
+        nc.sync.dma_start(w_words_raw[:].bitcast(I32), w1_words[0].bitcast(I32))
+        nc.gpsimd.memset(w_bytes_raw[:].bitcast(I32), 0)
+        for q in range(4):
+            nc.sync.dma_start(w_bytes_raw[32 * q : 32 * q + 4, :].bitcast(I32), w1_scales[0][4 * q : 4 * q + 4, :].bitcast(I32))
+
+        z_bf = [tile("z_bf%d" % part, [P, HALF, PACK], BF16) for part in range(2)]
+        pairs = []
+
+        def fetch_pairs(t):
+            pa = tile("pa%d" % t, [P, W], F32)
+            pb = tile("pb%d" % t, [P, W], F32)
+            nc.scalar.activation(pa[:], s_rows[t][:].indirect(n1_l[:]), COPY)
+            nc.scalar.activation(pb[:], s_rows[t][:].indirect(n2_l[:]), COPY)
+            ra = tile("ra%d" % t, [P, W], F32)
+            rb = tile("rb%d" % t, [P, W], F32)
+            nc.vector.tensor_tensor(ra[:], pa[:], pb[:], ALU.add)
+            nc.vector.scalar_tensor_tensor(rb[:], pa[:], 0.0625, pb[:], ALU.mult, ALU.mult)
+            pairs.append((ra, rb))
+
+        def put_pairs(t):
+            ra, rb = pairs[t]
+            dt = tile("dt%d" % t, [P, S], F32)
+            nc.scalar.activation(dt[:].indirect(n1_l[:]), ra[:], COPY)
+            nc.scalar.activation(dt[:].indirect(n2_l[:]), rb[:], COPY)
+            for part, cols in enumerate(HALVES):
+                nc.vector.tensor_scalar(z_bf[part][:, :, t], dt[:, cols], gn16[:, t : t + 1], None, ALU.mult)
+
+        fetch_pairs(0)
+        for t in range(PACK):
+            if t < LAST:
+                fetch_pairs(t + 1)
+            put_pairs(t)
+
+        w_codes = tile("w_codes", [P, 2 * N], U8)
+        nc.vector.tensor_copy(
+            w_codes[:].rearrange("p (t m b) -> p t m b", t=PACK, b=2), w_words_raw[:].rearrange("p (m t b) -> p t m b", t=PACK, b=2)
+        )
+        w_bytes = tile("w_bytes", [P, N], U8)
+        nc.vector.tensor_copy(w_bytes[:].rearrange("p (t m) -> p t m", t=PACK), w_bytes_raw[:].rearrange("p (m t) -> p t m", t=PACK))
+
+        z_codes = tile("z_codes", [P, S], U32)
+        z_bytes = tile("z_bytes", [P, S], U8)
+        for part, cols in enumerate(HALVES):
+            nc.vector.quantize_mx(z_codes[:, cols].bitcast(FP8X4), z_bytes[:, cols], z_bf[part][:].rearrange("p j t -> p (j t)"))
+
+        product(
+            "h", lambda t: w_codes[:, 2 * P * t : 2 * P * (t + 1)].bitcast(FP4X4), w_bytes, z_codes, z_bytes, h_rows, [(0, 0), (LAST, 0)]
+        )
+
+        y = tile("y", [P, PACK, S], F32)
+        y_bf = [tile("y_bf%d" % part, [P, HALF, PACK], BF16) for part in range(2)]
+        y_dram = out_0.rearrange("(p t) j -> p t j", t=PACK)
+        for t in range(PACK):
+            b1 = tile("b1_%d" % t, [P, S], F32)
+            b2 = tile("b2_%d" % t, [P, S], F32)
+            b3 = tile("b3_%d" % t, [P, S], F32)
+            nc.scalar.activation(b1[:], h_rows[t][:].indirect(n3_l[:]), COPY)
+            if t == 0:
+                nc.vector.tensor_copy(b2[:], h_rows[t][:].indirect(n4_l[:]))
+            else:
+                nc.scalar.activation(b2[:], h_rows[t][:].indirect(n4_l[:]), COPY)
+            nc.scalar.activation(b3[:], h_rows[t][:].indirect(n5_l[:]), COPY)
+            hi = tile("hi%d" % t, [P, S], F32)
+            lo = tile("lo%d" % t, [P, S], F32)
+            cap = tile("cap%d" % t, [P, S], F32)
+            top = tile("top%d" % t, [P, S], F32)
+            mid = tile("mid%d" % t, [P, S], F32)
+            spans = HALVES if t == LAST else (slice(0, S),)
+            for out, in0, in1, op in (
+                (hi, b1, b2, ALU.max), (lo, b1, b2, ALU.min), (cap, hi, b3, ALU.min), (top, hi, b3, ALU.max), (mid, lo, cap, ALU.max)
+            ):
+                for cols in spans:
+                    nc.vector.tensor_tensor(out[:, cols], in0[:, cols], in1[:, cols], op)
+            for cols in spans:
+                nc.vector.scalar_tensor_tensor(y[:, t, cols], mid[:, cols], -0.5, top[:, cols], ALU.mult, ALU.add)
+            nc.sync.dma_start(y_dram[:, t, :], y[:, t, :])
+            if t % 2 == 1:
+                for part, cols in enumerate(HALVES):
+                    rounded, exact = y_bf[part][:, :, t - 1 : t + 1], y[:, t - 1 : t + 1, cols].rearrange("p t j -> p j t")
+                    if t == LAST:
+                        nc.vector.tensor_copy(rounded, exact)
+                    else:
+                        nc.scalar.copy(rounded, exact)
+
+        y_codes = tile("y_codes", [P, S], U32)
+        y_bytes = tile("y_bytes", [P, S], U8)
+        for part, cols in enumerate(HALVES):
+            nc.vector.quantize_mx(y_codes[:, cols].bitcast(FP8X4), y_bytes[:, cols], y_bf[part][:].rearrange("p j t -> p (j t)"))
+        nc.scalar.dma_start(out_1[0].rearrange("p c r -> p (c r)").bitcast(I32), y_codes[:].bitcast(I32))
+        for q in range(4):
+            queue = nc.scalar if q == 3 else nc.sync
+            queue.dma_start(out_2[0][4 * q : 4 * q + 4, :].bitcast(I32), y_bytes[32 * q : 32 * q + 4, :].bitcast(I32))

@@ -46,34 +46,32 @@ def tile_picked_keybondtop2_none_po_kernel(
         d_byte_table = tile("d_byte_table", [P, G], U8)
         x_byte_table = tile("x_byte_table", [P, T], U8)
 
-        nc.gpsimd.memset(d_byte_table[:].bitcast(I32), 0)
-        nc.vector.memset(x_byte_table[:].bitcast(I32), 0)
         kidx_l = load_list("kidx_l", kidx)
+        for table, rows in ((d_byte_table, d_scales), (x_byte_table, x_scales)):
+            nc.scalar.dma_start(table[:].bitcast(I32), rows[0].bitcast(I32).unsqueeze(1).broadcast_to([16, 8, T // 4]))
+        for table, words in ((d_word_table, d_words), (x_word_table, x_words)):
+            nc.scalar.dma_start(table[:].bitcast(I32), words[0].rearrange("p c r -> p (c r)").bitcast(I32))
         gn_raw = tile("gn_raw", [P, PACK], F32)
         nc.scalar.dma_start(gn_raw[:], gn.rearrange("(p t) o -> p (t o)", t=PACK))
-        for a in range(2):
-            nc.scalar.dma_start(d_byte_table[a:P:16, :].bitcast(I32), d_scales[0][a:16:2, :].bitcast(I32))
-        for q in range(4):
-            nc.scalar.dma_start(x_byte_table[32 * q : 32 * q + 4, :].bitcast(I32), x_scales[0][4 * q : 4 * q + 4, :].bitcast(I32))
         offs_l = load_list("offs_l", offs)
-        nc.sync.dma_start(d_word_table[:].bitcast(I32), d_words[0].rearrange("p c r -> p (c r)").bitcast(I32))
         n1_l = load_list("n1_l", n1)
         n2_l = load_list("n2_l", n2)
-        nc.sync.dma_start(x_word_table[:].bitcast(I32), x_words[0].rearrange("p c r -> p (c r)").bitcast(I32))
         n3_l = load_list("n3_l", n3)
         n4_l = load_list("n4_l", n4)
         n5_l = load_list("n5_l", n5)
 
-        d_bytes_picked = tile("d_bytes_picked", [P, H], U8)
-        nc.vector.tensor_copy(d_bytes_picked[:], d_byte_table[:].indirect(kidx_l[:]))
-        d_bytes_dealt = tile("d_bytes_dealt", [P, H], U8)
+        bytes_picked = tile("bytes_picked", [P, H + S], U8)
+        nc.vector.tensor_copy(bytes_picked[:, :H], d_byte_table[:].indirect(kidx_l[:]))
+        nc.vector.tensor_copy(bytes_picked[:, H:], x_byte_table[:].indirect(offs_l[:]))
+        bytes_dealt = tile("bytes_dealt", [P, H + S], U8)
         nc.vector.tensor_copy(
-            d_bytes_dealt[:].rearrange("p (t m) -> p t m", t=PACK), d_bytes_picked[:].rearrange("p (m t) -> p t m", t=PACK)
+            bytes_dealt[:, :H].rearrange("p (t m) -> p t m", t=PACK), bytes_picked[:, :H].rearrange("p (m t) -> p t m", t=PACK)
         )
-        d_bytes = tile("d_bytes", [P, H], U8, "d_bytes_then_w_bytes")
-        nc.vector.tensor_copy(d_bytes[:].bitcast(I32), d_bytes_dealt[:].bitcast(I32))
-        for a in range(2):
-            nc.sync.dma_start(d_bytes[2 + a : P : 32, :].bitcast(I32), d_bytes_dealt[16 + a : P : 32, :].bitcast(I32))
+        nc.vector.tensor_copy(bytes_dealt[:, H:].bitcast(I32), bytes_picked[:, H:].bitcast(I32))
+        dx_bytes = tile("dx_bytes", [P, H + S], U8, "d_bytes_then_w_bytes")
+        nc.vector.tensor_copy(dx_bytes[:].bitcast(I32), bytes_dealt[:].bitcast(I32))
+        for a in range(1, 4):
+            nc.sync.dma_start(dx_bytes[a:P:32, :].bitcast(I32), bytes_dealt[8 * a : P : 32, :].bitcast(I32))
 
         d_words_picked = tile("d_words_picked", [P, H], U32)
         nc.vector.tensor_copy(d_words_picked[:], d_word_table[:].indirect(kidx_l[:]))
@@ -82,8 +80,6 @@ def tile_picked_keybondtop2_none_po_kernel(
             d_codes[:].bitcast(I32).rearrange("p (t m) -> p t m", t=PACK),
             d_words_picked[:].bitcast(I32).rearrange("p (m t) -> p t m", t=PACK),
         )
-        x_bytes = tile("x_bytes", [P, S], U8)
-        nc.vector.tensor_copy(x_bytes[:], x_byte_table[:].indirect(offs_l[:]))
         x_codes = tile("x_codes", [P, S], U32)
         nc.vector.tensor_copy(x_codes[:], x_word_table[:].indirect(offs_l[:]))
 
@@ -109,7 +105,7 @@ def tile_picked_keybondtop2_none_po_kernel(
                         nc.vector.tensor_copy(rows[t][:, cols], bank[:])
 
         s_rows = [tile("s_rows%d" % t, [P, S], F32) for t in range(PACK)]
-        product("s", lambda t: d_codes[:, P * t : P * (t + 1)].bitcast(FP8X4), d_bytes, x_codes, x_bytes, s_rows, [(0, 0)])
+        product("s", lambda t: d_codes[:, P * t : P * (t + 1)].bitcast(FP8X4), dx_bytes[:, :H], x_codes, dx_bytes[:, H:], s_rows, [(0, 0)])
 
         w_words_raw = tile("w_words_raw", [P, 2 * N], U8, "x_table_then_w_words")
         w_bytes_raw = tile("w_bytes_raw", [P, N], U8, "d_bytes_then_w_bytes")
@@ -189,14 +185,11 @@ def tile_picked_keybondtop2_none_po_kernel(
             for cols in spans:
                 nc.vector.scalar_tensor_tensor(y[:, t, cols], mid[:, cols], -0.5, top[:, cols], ALU.mult, ALU.add)
             nc.sync.dma_start(y_dram[:, t, :], y[:, t, :])
-            if t % 2 == 1:
-                for part, cols in enumerate(HALVES):
-                    rounded, exact = y_bf[part][:, :, t - 1 : t + 1], y[:, t - 1 : t + 1, cols].rearrange("p t j -> p j t")
-                    if t == LAST:
-                        nc.vector.tensor_copy(rounded, exact)
-                    else:
-                        nc.scalar.copy(rounded, exact)
 
+        for part, cols in enumerate(HALVES):
+            nc.vector.tensor_copy(
+                y_bf[part][:].rearrange("p (c i) t -> p c t i", i=4), y[:, :, cols].rearrange("p t (c i) -> p c t i", i=4)
+            )
         y_codes = tile("y_codes", [P, S], U32)
         y_bytes = tile("y_bytes", [P, S], U8)
         for part, cols in enumerate(HALVES):

@@ -42,7 +42,7 @@ def tile_picked_keybondtop2_none_po_kernel(
             return held
 
         d_word_table = tile("d_word_table", [P, G], U32)
-        x_word_table = tile("x_word_table", [P, T], U32, "x_table_then_w_words")
+        x_word_table = tile("x_word_table", [P, T], U32, "x_table_then_w_codes")
         d_byte_table = tile("d_byte_table", [P, G], U8)
         x_byte_table = tile("x_byte_table", [P, T], U8)
 
@@ -63,17 +63,17 @@ def tile_picked_keybondtop2_none_po_kernel(
         bytes_picked = tile("bytes_picked", [P, H + S], U8)
         nc.vector.tensor_copy(bytes_picked[:, :H], d_byte_table[:].indirect(kidx_l[:]))
         nc.vector.tensor_copy(bytes_picked[:, H:], x_byte_table[:].indirect(offs_l[:]))
-        bytes_dealt = tile("bytes_dealt", [P, H + S], U8)
+        bytes_dealt = tile("bytes_dealt", [P, H + S], U8, "w_words")
         nc.vector.tensor_copy(
             bytes_dealt[:, :H].rearrange("p (t m) -> p t m", t=PACK), bytes_picked[:, :H].rearrange("p (m t) -> p t m", t=PACK)
         )
         nc.vector.tensor_copy(bytes_dealt[:, H:].bitcast(I32), bytes_picked[:, H:].bitcast(I32))
-        dx_bytes = tile("dx_bytes", [P, H + S], U8, "d_bytes_then_w_bytes")
+        dx_bytes = tile("dx_bytes", [P, H + S], U8, "dx_bytes_then_w_bytes")
         nc.vector.tensor_copy(dx_bytes[:].bitcast(I32), bytes_dealt[:].bitcast(I32))
         for a in range(1, 4):
             nc.sync.dma_start(dx_bytes[a:P:32, :].bitcast(I32), bytes_dealt[8 * a : P : 32, :].bitcast(I32))
 
-        d_words_picked = tile("d_words_picked", [P, H], U32)
+        d_words_picked = tile("d_words_picked", [P, H], U32, "w_raw_bytes")
         nc.vector.tensor_copy(d_words_picked[:], d_word_table[:].indirect(kidx_l[:]))
         d_codes = tile("d_codes", [P, H], U32)
         nc.vector.tensor_copy(
@@ -107,8 +107,8 @@ def tile_picked_keybondtop2_none_po_kernel(
         s_rows = [tile("s_rows%d" % t, [P, S], F32) for t in range(PACK)]
         product("s", lambda t: d_codes[:, P * t : P * (t + 1)].bitcast(FP8X4), dx_bytes[:, :H], x_codes, dx_bytes[:, H:], s_rows, [(0, 0)])
 
-        w_words_raw = tile("w_words_raw", [P, 2 * N], U8, "x_table_then_w_words")
-        w_bytes_raw = tile("w_bytes_raw", [P, N], U8, "d_bytes_then_w_bytes")
+        w_words_raw = tile("w_words_raw", [P, 2 * N], U8, "w_words")
+        w_bytes_raw = tile("w_bytes_raw", [P, N], U8, "w_raw_bytes")
         nc.sync.dma_start(w_words_raw[:].bitcast(I32), w1_words[0].bitcast(I32))
         nc.gpsimd.memset(w_bytes_raw[:].bitcast(I32), 0)
         for q in range(4):
@@ -122,8 +122,8 @@ def tile_picked_keybondtop2_none_po_kernel(
             pb = tile("pb%d" % t, [P, W], F32)
             nc.scalar.activation(pa[:], s_rows[t][:].indirect(n1_l[:]), COPY)
             nc.scalar.activation(pb[:], s_rows[t][:].indirect(n2_l[:]), COPY)
-            ra = tile("ra%d" % t, [P, W], F32)
-            rb = tile("rb%d" % t, [P, W], F32)
+            ra = tile("ra%d" % t, [P, W], F32, "w_words" if t == LAST else None)
+            rb = tile("rb%d" % t, [P, W], F32, "w_raw_bytes" if t == LAST else None)
             nc.vector.tensor_tensor(ra[:], pa[:], pb[:], ALU.add)
             nc.vector.scalar_tensor_tensor(rb[:], pa[:], 0.0625, pb[:], ALU.mult, ALU.mult)
             pairs.append((ra, rb))
@@ -137,17 +137,20 @@ def tile_picked_keybondtop2_none_po_kernel(
                 nc.vector.tensor_scalar(z_bf[part][:, :, t], dt[:, cols], gn16[:, t : t + 1], None, ALU.mult)
 
         fetch_pairs(0)
-        for t in range(PACK):
-            if t < LAST:
-                fetch_pairs(t + 1)
+        for t in range(LAST - 1):
+            fetch_pairs(t + 1)
             put_pairs(t)
 
-        w_codes = tile("w_codes", [P, 2 * N], U8)
+        w_codes = tile("w_codes", [P, 2 * N], U8, "x_table_then_w_codes")
         nc.vector.tensor_copy(
             w_codes[:].rearrange("p (t m b) -> p t m b", t=PACK, b=2), w_words_raw[:].rearrange("p (m t b) -> p t m b", t=PACK, b=2)
         )
-        w_bytes = tile("w_bytes", [P, N], U8)
+        w_bytes = tile("w_bytes", [P, N], U8, "dx_bytes_then_w_bytes")
         nc.vector.tensor_copy(w_bytes[:].rearrange("p (t m) -> p t m", t=PACK), w_bytes_raw[:].rearrange("p (m t) -> p t m", t=PACK))
+
+        fetch_pairs(LAST)
+        put_pairs(LAST - 1)
+        put_pairs(LAST)
 
         z_codes = tile("z_codes", [P, S], U32)
         z_bytes = tile("z_bytes", [P, S], U8)
@@ -171,8 +174,8 @@ def tile_picked_keybondtop2_none_po_kernel(
             else:
                 nc.scalar.activation(b2[:], h_rows[t][:].indirect(n4_l[:]), COPY)
             nc.scalar.activation(b3[:], h_rows[t][:].indirect(n5_l[:]), COPY)
-            hi = tile("hi%d" % t, [P, S], F32)
-            lo = tile("lo%d" % t, [P, S], F32)
+            hi = tile("hi%d" % t, [P, S], F32, "hi")
+            lo = tile("lo%d" % t, [P, S], F32, "lo")
             cap = tile("cap%d" % t, [P, S], F32)
             top = tile("top%d" % t, [P, S], F32)
             mid = tile("mid%d" % t, [P, S], F32)
@@ -187,9 +190,8 @@ def tile_picked_keybondtop2_none_po_kernel(
             nc.sync.dma_start(y_dram[:, t, :], y[:, t, :])
 
         for part, cols in enumerate(HALVES):
-            nc.vector.tensor_copy(
-                y_bf[part][:].rearrange("p (c i) t -> p c t i", i=4), y[:, :, cols].rearrange("p t (c i) -> p c t i", i=4)
-            )
+            rounding_copy = nc.scalar.copy if part == 0 else nc.vector.tensor_copy
+            rounding_copy(y_bf[part][:].rearrange("p (c i) t -> p c t i", i=4), y[:, :, cols].rearrange("p t (c i) -> p c t i", i=4))
         y_codes = tile("y_codes", [P, S], U32)
         y_bytes = tile("y_bytes", [P, S], U8)
         for part, cols in enumerate(HALVES):

@@ -173,18 +173,22 @@ def tile_picked_keybondtop2_none_po_kernel(
                 nc.vector.tensor_copy(b2[:], h_rows[t][:].indirect(n4_l[:]))
             else:
                 nc.scalar.activation(b2[:], h_rows[t][:].indirect(n4_l[:]), COPY)
-            nc.scalar.activation(b3[:], h_rows[t][:].indirect(n5_l[:]), COPY)
+            spans = HALVES if t == LAST else (slice(0, S),)
+            for cols in spans:
+                nc.scalar.activation(b3[:, cols], h_rows[t][:].indirect(n5_l[:, cols.start // 16 : cols.stop // 16]), COPY)
             hi = tile("hi%d" % t, [P, S], F32, "hi")
             lo = tile("lo%d" % t, [P, S], F32, "lo")
             cap = tile("cap%d" % t, [P, S], F32)
             top = tile("top%d" % t, [P, S], F32)
             mid = tile("mid%d" % t, [P, S], F32)
-            spans = HALVES if t == LAST else (slice(0, S),)
-            for out, in0, in1, op in (
-                (hi, b1, b2, ALU.max), (lo, b1, b2, ALU.min), (cap, hi, b3, ALU.min), (top, hi, b3, ALU.max), (mid, lo, cap, ALU.max)
-            ):
+            for out, op in ((hi, ALU.max), (lo, ALU.min)):
                 for cols in spans:
-                    nc.vector.tensor_tensor(out[:, cols], in0[:, cols], in1[:, cols], op)
+                    nc.vector.tensor_tensor(out[:, cols], b1[:, cols], b2[:, cols], op)
+            for cols in spans:
+                nc.vector.tensor_tensor(cap[:, cols], hi[:, cols], b3[:, cols], ALU.min)
+                nc.vector.tensor_tensor(top[:, cols], hi[:, cols], b3[:, cols], ALU.max)
+            for cols in spans:
+                nc.vector.tensor_tensor(mid[:, cols], lo[:, cols], cap[:, cols], ALU.max)
             for cols in spans:
                 nc.vector.scalar_tensor_tensor(y[:, t, cols], mid[:, cols], -0.5, top[:, cols], ALU.mult, ALU.add)
             nc.sync.dma_start(y_dram[:, t, :], y[:, t, :])

from contextlib import ExitStack

import concourse.mybir as mybir

K, T, S, N, G, H, W = 512, 2048, 256, 512, 2048, 512, 128
P = 128
PACK = 4
FLOPS = 2 * K * H * S + 2 * H * N * S

F32 = mybir.dt.float32
BF16 = mybir.dt.bfloat16
I32 = mybir.dt.int32
U32 = mybir.dt.uint32
U16 = mybir.dt.uint16
U8 = mybir.dt.uint8
FP8X4 = mybir.dt.float8_e4m3fn_x4
FP4X4 = mybir.dt.float4_e2m1fn_x4
ALU = mybir.AluOpType
COPY = mybir.ActivationFunctionType.Copy

H_WINDOW = 352
HALF = S // 2
HALVES = (slice(0, HALF), slice(HALF, S))
LAST = PACK - 1


def tile_picked_keybondtop2_none_po_kernel(
    tc, x_words, x_scales, d_words, d_scales, gn, w1_words, w1_scales, offs, kidx, n1, n2, n3, n4, n5, out_0, out_1, out_2
):
    nc = tc.nc
    with ExitStack() as ctx:
        lists = ctx.enter_context(tc.tile_pool(name="lists", bufs=1))
        sb = ctx.enter_context(tc.tile_pool(name="sb", bufs=1))
        ps = ctx.enter_context(tc.psum_pool(name="ps", bufs=1))

        def tile(name, shape, dtype, tag=None):
            return sb.tile(shape, dtype, name=name, tag=tag or name, align_bytes=64)

        def load_list(name, dram):
            held = lists.tile(list(dram.shape), U16, name=name)
            nc.sync.dma_start(held[:], dram)
            return held

        d_word_table = tile("d_word_table", [P, G], U32)
        x_word_table = tile("x_word_table", [P, T], U32, "x_table_then_w_codes")
        d_byte_table = tile("d_byte_table", [P, G], U8)
        x_byte_table = tile("x_byte_table", [P, T], U8)

        kidx_l = load_list("kidx_l", kidx)
        for table, rows in ((d_byte_table, d_scales), (x_byte_table, x_scales)):
            nc.scalar.dma_start(table[:].bitcast(I32), rows[0].bitcast(I32).unsqueeze(1).broadcast_to([16, 8, T // 4]))
        for table, words in ((d_word_table, d_words), (x_word_table, x_words)):
            nc.scalar.dma_start(table[:].bitcast(I32), words[0].rearrange("p c r -> p (c r)").bitcast(I32))
        gn_raw = tile("gn_raw", [P, PACK], F32)
        nc.scalar.dma_start(gn_raw[:], gn.rearrange("(p t) o -> p (t o)", t=PACK))
        offs_l = load_list("offs_l", offs)
        n1_l = load_list("n1_l", n1)
        n2_l = load_list("n2_l", n2)
        n3_l = load_list("n3_l", n3)
        n4_l = load_list("n4_l", n4)
        n5_l = load_list("n5_l", n5)

        bytes_picked = tile("bytes_picked", [P, H + S], U8)
        nc.vector.tensor_copy(bytes_picked[:, :H], d_byte_table[:].indirect(kidx_l[:]))
        nc.vector.tensor_copy(bytes_picked[:, H:], x_byte_table[:].indirect(offs_l[:]))
        bytes_dealt = tile("bytes_dealt", [P, H + S], U8, "w_words")
        nc.vector.tensor_copy(
            bytes_dealt[:, :H].rearrange("p (t m) -> p t m", t=PACK), bytes_picked[:, :H].rearrange("p (m t) -> p t m", t=PACK)
        )
        nc.vector.tensor_copy(bytes_dealt[:, H:].bitcast(I32), bytes_picked[:, H:].bitcast(I32))
        dx_bytes = tile("dx_bytes", [P, H + S], U8, "dx_bytes_then_w_bytes")
        nc.vector.tensor_copy(dx_bytes[:].bitcast(I32), bytes_dealt[:].bitcast(I32))
        for a in range(1, 4):
            nc.sync.dma_start(dx_bytes[a:P:32, :].bitcast(I32), bytes_dealt[8 * a : P : 32, :].bitcast(I32))

        d_words_picked = tile("d_words_picked", [P, H], U32, "w_raw_bytes")
        nc.vector.tensor_copy(d_words_picked[:], d_word_table[:].indirect(kidx_l[:]))
        d_codes = tile("d_codes", [P, H], U32)
        nc.vector.tensor_copy(
            d_codes[:].bitcast(I32).rearrange("p (t m) -> p t m", t=PACK),
            d_words_picked[:].bitcast(I32).rearrange("p (m t) -> p t m", t=PACK),
        )
        x_codes = tile("x_codes", [P, S], U32)
        nc.vector.tensor_copy(x_codes[:], x_word_table[:].indirect(offs_l[:]))

        gn16 = tile("gn16", [P, PACK], F32)
        nc.scalar.activation(gn16[:], gn_raw[:], COPY, scale=0.0625)

        h_rows = [tile("h_rows%d" % t, [P, H_WINDOW], F32) for t in range(PACK)]
        for t in range(PACK):
            nc.gpsimd.memset(h_rows[t][:, S:], 0.0)

        def product(name, lhs_codes, lhs_bytes, rhs_codes, rhs_bytes, rows, on_scalar):
            for t in range(PACK):
                for part, cols in enumerate(HALVES if t == 0 else (slice(0, S),)):
                    tag = "first%d" % part if t == 0 else "%s%d" % (name, t)
                    bank = ps.tile([P, cols.stop - cols.start], F32, name="%s_bank%d_%d" % (name, t, part), tag=tag)
                    nc.tensor.matmul_mx(
                        bank[:], lhsT=lhs_codes(t), lhsT_scale=lhs_bytes[:, P * t : P * (t + 1)],
                        rhs=rhs_codes[:, cols].bitcast(FP8X4), rhs_scale=rhs_bytes[:, cols], start=True, stop=True,
                    )
                    if (t, part) in on_scalar:
                        nc.scalar.copy(rows[t][:, cols], bank[:])
                    else:
                        nc.vector.tensor_copy(rows[t][:, cols], bank[:])

        s_rows = [tile("s_rows%d" % t, [P, S], F32) for t in range(PACK)]
        product("s", lambda t: d_codes[:, P * t : P * (t + 1)].bitcast(FP8X4), dx_bytes[:, :H], x_codes, dx_bytes[:, H:], s_rows, [(0, 0)])

        w_words_raw = tile("w_words_raw", [P, 2 * N], U8, "w_words")
        w_bytes_raw = tile("w_bytes_raw", [P, N], U8, "w_raw_bytes")
        nc.sync.dma_start(w_words_raw[:].bitcast(I32), w1_words[0].bitcast(I32))
        nc.gpsimd.memset(w_bytes_raw[:].bitcast(I32), 0)
        for q in range(4):
            nc.sync.dma_start(w_bytes_raw[32 * q : 32 * q + 4, :].bitcast(I32), w1_scales[0][4 * q : 4 * q + 4, :].bitcast(I32))

        z_bf = [tile("z_bf%d" % part, [P, HALF, PACK], BF16) for part in range(2)]
        pairs = []

        def fetch_pairs(t):
            pa = tile("pa%d" % t, [P, W], F32)
            pb = tile("pb%d" % t, [P, W], F32)
            nc.scalar.activation(pa[:], s_rows[t][:].indirect(n1_l[:]), COPY)
            nc.scalar.activation(pb[:], s_rows[t][:].indirect(n2_l[:]), COPY)
            ra = tile("ra%d" % t, [P, W], F32, "w_words" if t == LAST else None)
            rb = tile("rb%d" % t, [P, W], F32, "w_raw_bytes" if t == LAST else None)
            nc.vector.tensor_tensor(ra[:], pa[:], pb[:], ALU.add)
            nc.vector.scalar_tensor_tensor(rb[:], pa[:], 0.0625, pb[:], ALU.mult, ALU.mult)
            pairs.append((ra, rb))

        def put_pairs(t):
            ra, rb = pairs[t]
            dt = tile("dt%d" % t, [P, S], F32)
            nc.scalar.activation(dt[:].indirect(n1_l[:]), ra[:], COPY)
            nc.scalar.activation(dt[:].indirect(n2_l[:]), rb[:], COPY)
            for part, cols in enumerate(HALVES):
                nc.vector.tensor_scalar(z_bf[part][:, :, t], dt[:, cols], gn16[:, t : t + 1], None, ALU.mult)

        fetch_pairs(0)
        for t in range(LAST - 1):
            fetch_pairs(t + 1)
            put_pairs(t)

        w_codes = tile("w_codes", [P, 2 * N], U8, "x_table_then_w_codes")
        nc.vector.tensor_copy(
            w_codes[:].rearrange("p (t m b) -> p t m b", t=PACK, b=2), w_words_raw[:].rearrange("p (m t b) -> p t m b", t=PACK, b=2)
        )
        w_bytes = tile("w_bytes", [P, N], U8, "dx_bytes_then_w_bytes")
        nc.vector.tensor_copy(w_bytes[:].rearrange("p (t m) -> p t m", t=PACK), w_bytes_raw[:].rearrange("p (m t) -> p t m", t=PACK))

        fetch_pairs(LAST)
        put_pairs(LAST - 1)
        put_pairs(LAST)

        z_codes = tile("z_codes", [P, S], U32)
        z_bytes = tile("z_bytes", [P, S], U8)
        for part, cols in enumerate(HALVES):
            nc.vector.quantize_mx(z_codes[:, cols].bitcast(FP8X4), z_bytes[:, cols], z_bf[part][:].rearrange("p j t -> p (j t)"))

        product(
            "h", lambda t: w_codes[:, 2 * P * t : 2 * P * (t + 1)].bitcast(FP4X4), w_bytes, z_codes, z_bytes, h_rows, [(0, 0), (LAST, 0)]
        )

        y = tile("y", [P, PACK, S], F32)
        y_bf = [tile("y_bf%d" % part, [P, HALF, PACK], BF16) for part in range(2)]
        y_dram = out_0.rearrange("(p t) j -> p t j", t=PACK)
        for t in range(PACK):
            b1 = tile("b1_%d" % t, [P, S], F32)
            b2 = tile("b2_%d" % t, [P, S], F32)
            b3 = tile("b3_%d" % t, [P, S], F32)
            nc.scalar.activation(b1[:], h_rows[t][:].indirect(n3_l[:]), COPY)
            if t == 0:
                nc.vector.tensor_copy(b2[:], h_rows[t][:].indirect(n4_l[:]))
            else:
                nc.scalar.activation(b2[:], h_rows[t][:].indirect(n4_l[:]), COPY)
            spans = HALVES if t == LAST else (slice(0, S),)
            for cols in spans:
                nc.scalar.activation(b3[:, cols], h_rows[t][:].indirect(n5_l[:, cols.start // 16 : cols.stop // 16]), COPY)
            hi = tile("hi%d" % t, [P, S], F32, "hi")
            lo = tile("lo%d" % t, [P, S], F32, "lo")
            cap = tile("cap%d" % t, [P, S], F32)
            top = tile("top%d" % t, [P, S], F32)
            mid = tile("mid%d" % t, [P, S], F32)
            for out, op in ((hi, ALU.max), (lo, ALU.min)):
                for cols in spans:
                    nc.vector.tensor_tensor(out[:, cols], b1[:, cols], b2[:, cols], op)
            for cols in spans:
                nc.vector.tensor_tensor(cap[:, cols], hi[:, cols], b3[:, cols], ALU.min)
                nc.vector.tensor_tensor(top[:, cols], hi[:, cols], b3[:, cols], ALU.max)
            for cols in spans:
                nc.vector.tensor_tensor(mid[:, cols], lo[:, cols], cap[:, cols], ALU.max)
            for cols in spans:
                nc.vector.scalar_tensor_tensor(y[:, t, cols], mid[:, cols], -0.5, top[:, cols], ALU.mult, ALU.add)
            nc.sync.dma_start(y_dram[:, t, :], y[:, t, :])

        for part, cols in enumerate(HALVES):
            rounding_copy = nc.scalar.copy if part == 0 else nc.vector.tensor_copy
            rounding_copy(y_bf[part][:].rearrange("p (c i) t -> p c t i", i=4), y[:, :, cols].rearrange("p t (c i) -> p c t i", i=4))
        y_codes = tile("y_codes", [P, S], U32)
        y_bytes = tile("y_bytes", [P, S], U8)
        for part, cols in enumerate(HALVES):
            nc.vector.quantize_mx(y_codes[:, cols].bitcast(FP8X4), y_bytes[:, cols], y_bf[part][:].rearrange("p j t -> p (j t)"))
        nc.scalar.dma_start(out_1[0].rearrange("p c r -> p (c r)").bitcast(I32), y_codes[:].bitcast(I32))
        for q in range(4):
            queue = nc.scalar if q == 3 else nc.sync
            queue.dma_start(out_2[0][4 * q : 4 * q + 4, :].bitcast(I32), y_bytes[32 * q : 32 * q + 4, :].bitcast(I32))
